import numpy as np
import ml_dtypes


def mxq(x, axis, fmt="e4m3"):
    dtype, down = {"e4m3": (ml_dtypes.float8_e4m3fn, 7), "e5m2": (ml_dtypes.float8_e5m2, 14)}[fmt]
    v = np.moveaxis(np.asarray(x, np.float32).astype(ml_dtypes.bfloat16).astype(np.float64), axis, -1)
    blocks = v.reshape(v.shape[:-1] + (-1, 32))
    amax = np.abs(blocks).max(-1, keepdims=True)
    byte = np.maximum(np.where(amax > 0, np.frexp(amax)[1] - 1 + 127, 0) - down, 1)
    scale = np.exp2(byte - 127.0)
    codes = (blocks / scale).astype(np.float32).astype(dtype).astype(np.float64)
    return np.moveaxis((codes * scale).reshape(v.shape), -1, axis)


WIDE = False


def mx_kscale(k):
    if not WIDE:
        return np.ones(k)
    levels = np.array([10, -10, 5, -5, 0])
    if k % 512:
        return np.exp2(np.random.permutation(np.resize(levels, k // 32))).repeat(32)
    a = np.empty((k // 512, 16))
    for p in range(k // 512):
        a[p, :8] = np.random.permutation(np.resize(levels, 8))
        for g in range(8):
            far = levels[np.abs(levels - a[p, g]) >= 10]
            a[p, g + 8] = far[np.random.randint(len(far))]
    return np.exp2(a.ravel()).repeat(32)


def f64(x):
    return np.asarray(x).astype(np.float64)


def striped(idx):
    return np.tile(idx.reshape(-1, 16).T, (8, 1)).astype(np.uint16)


def unstriped(offs):
    return offs[:16].T.reshape(-1).astype(np.int64)


def striped8(idx):
    return np.concatenate([x.reshape(-1, 16).T for x in idx]).astype(np.uint16)


def runs(offs, k):
    lists = np.stack([offs[16 * r : 16 * r + 16].T.reshape(-1) for r in range(8)]).astype(np.int64)
    return lists[np.arange(k) % 512 // 64]


def pack_weight(w):
    k, n = w.shape
    w = f64(np.asarray(w, np.float32).astype(ml_dtypes.bfloat16)).reshape(k // 32, 32, n)
    amax = np.abs(w).max(1)
    byte = np.clip(np.where(amax > 0, np.frexp(amax)[1] - 1 + 127 - 7, 1), 1, 254)
    scaled = (w * np.exp2(127.0 - byte)[:, None, :]).reshape(k, n).astype(np.float32)
    words = np.ascontiguousarray(scaled.reshape(k // 512, 128, 4, n).transpose(0, 1, 3, 2)).astype(ml_dtypes.float8_e4m3fn).view(np.uint8)
    return words, np.ascontiguousarray(byte.astype(np.uint8).reshape(k // 512, 16, n))


def unpack_weight(words, scales):
    g, p, n, _ = words.shape
    vals = np.ascontiguousarray(words).view(ml_dtypes.float8_e4m3fn).astype(np.float64) * np.repeat(np.exp2(scales.astype(np.float64) - 127.0), 8, axis=1)[..., None]
    return vals.transpose(0, 1, 3, 2).reshape(g * 512, n)


E2M1 = np.array([0.0, 0.5, 1.0, 1.5, 2.0, 3.0, 4.0, 6.0, -0.0, -0.5, -1.0, -1.5, -2.0, -3.0, -4.0, -6.0])


def pack_fp4(w):
    k, n = w.shape
    w = f64(np.asarray(w, np.float32).astype(ml_dtypes.bfloat16)).reshape(k // 32, 32, n)
    amax = np.abs(w).max(1)
    mant, ex = np.frexp(amax / 6.0)
    byte = np.clip(np.where(amax > 0, np.where(mant > 0.5, ex, ex - 1) + 127, 1), 1, 254)
    scaled = (w * np.exp2(127.0 - byte)[:, None, :]).reshape(k, n).astype(np.float32)
    c = np.ascontiguousarray(scaled.reshape(k // 512, 128, 4, n).transpose(0, 1, 3, 2)).astype(ml_dtypes.float4_e2m1fn).view(np.uint8) & 0xF
    words = (c[..., 0::2] | (c[..., 1::2] << 4)).reshape(k // 512, 128, 2 * n)
    return np.ascontiguousarray(words), np.ascontiguousarray(byte.astype(np.uint8).reshape(k // 512, 16, n))


def unpack_fp4(words, scales):
    g, _, n = scales.shape
    words = np.ascontiguousarray(words).reshape(g, 128, n, 2)
    nib = np.empty((g, 128, n, 4), np.uint8)
    nib[..., 0::2] = words & 0xF
    nib[..., 1::2] = words >> 4
    vals = E2M1[nib] * np.repeat(np.exp2(scales.astype(np.float64) - 127.0), 8, axis=1)[..., None]
    return vals.transpose(0, 1, 3, 2).reshape(g * 512, n)


def sigmoid(v):
    return 1.0 / (1.0 + np.exp(-np.maximum(v, -700.0)))

def planes(y):
    n, m = y.shape
    v = y.astype(np.float32).astype(ml_dtypes.bfloat16).astype(np.float64).reshape(n // 32, 32, m)
    top = np.abs(v).max(1)
    byte = np.clip(np.where(top > 0, np.frexp(top)[1] - 1 + 127 - 7, 1), 1, 254)
    codes = (v * np.exp2(127.0 - byte)[:, None, :]).reshape(n, m).astype(np.float32).astype(ml_dtypes.float8_e4m3fn).view(np.uint8)
    words = codes.reshape(n // 512, 128, 4, m).transpose(0, 1, 3, 2)
    return np.ascontiguousarray(words), np.ascontiguousarray(byte.astype(np.uint8).reshape(n // 512, 16, m))


K, T, S, N, H, W = 512, 2048, 512, 512, 512, 256


def setup_inputs():
    n = np.random.standard_normal
    s = mx_kscale(K)[:, None]
    u = mx_kscale(H)
    packed_xT = pack_weight(n((K, T)) * s)
    packed_w1 = pack_fp4(n((K, H)) / np.sqrt(K) / s)
    packed_w2 = pack_fp4(n((H, N)) / np.sqrt(H) / u[:, None])
    perm = np.stack([np.random.permutation(S) for _ in range(8)])
    return {
        "x_words": packed_xT[0],
        "x_scales": packed_xT[1],
        "w1_words": packed_w1[0],
        "w1_scales": packed_w1[1],
        "gn": (np.random.uniform(0.5, 1.5, (H, 1)) * u[:, None]).astype(np.float32),
        "w2_words": packed_w2[0],
        "w2_scales": packed_w2[1],
        "offs": striped(np.random.permutation(T)[:S]),
        "n1": striped8(perm[:, :W]),
        "n2": striped8(perm[:, W:]),
        "n3": striped8(np.stack([np.random.permutation(S) for _ in range(8)])),
        "n4": striped8(np.stack([np.random.permutation(S) for _ in range(8)])),
    }


def reference(x_words, x_scales, w1_words, w1_scales, gn, w2_words, w2_scales, offs, n1, n2, n3, n4):
    xq = unpack_weight(x_words, x_scales)[:, unstriped(offs)]
    y = unpack_fp4(w1_words, w1_scales).T @ xq
    pa = y[np.arange(H)[:, None], runs(n1, H)]
    pb = y[np.arange(H)[:, None], runs(n2, H)]
    ra = pa * sigmoid(pb)
    ds = y.copy()
    ds[np.arange(H)[:, None], runs(n2, H)] = ra
    z = f64(gn) * ds
    h = unpack_fp4(w2_words, w2_scales).T @ mxq(z, 0, "e4m3")
    out_0 = 0.75 * (h * (y[np.arange(H)[:, None], runs(n4, H)]) - ((h[np.arange(N)[:, None], runs(n3, N)]) * y))
    return (out_0,) + planes(out_0)

@@ -1,0 +1,263 @@
+from contextlib import ExitStack
+
+import concourse.mybir as mybir
+
+F32 = mybir.dt.float32
+BF16 = mybir.dt.bfloat16
+I32 = mybir.dt.int32
+U32 = mybir.dt.uint32
+U16 = mybir.dt.uint16
+U8 = mybir.dt.uint8
+FP8X4 = mybir.dt.float8_e4m3fn_x4
+FP4X4 = mybir.dt.float4_e2m1fn_x4
+MULT = mybir.AluOpType.mult
+SUB = mybir.AluOpType.subtract
+COPY = mybir.ActivationFunctionType.Copy
+SIGMOID = mybir.ActivationFunctionType.Sigmoid
+
+P = 128
+T = 2048
+S = 512
+W = 256
+HALF = 256
+FLOPS = 2 * 2 * 512 * 512 * 512
+OUT_CHUNKS = ((0, 256), (256, 384), (384, 512))
+
+
+def tile_picked_skipcrossbfold_none_po_kernel(
+    tc, x_words, x_scales, w1_words, w1_scales, gn, w2_words, w2_scales, offs, n1, n2, n3, n4, out_0, out_1, out_2
+):
+    nc = tc.nc
+    with ExitStack() as ctx:
+        lists = ctx.enter_context(tc.tile_pool(name="lists", bufs=1))
+        sb = ctx.enter_context(tc.tile_pool(name="sb", bufs=1))
+        ps = ctx.enter_context(tc.psum_pool(name="ps", bufs=1))
+
+        def sbt(shape, dtype, name, tag=None):
+            return sb.tile(shape, dtype, name=name, tag=tag or name, align_bytes=64)
+
+        def entries(lst, a, b):
+            return lst[:, a // 16 : b // 16]
+
+        def load_scale_rows(queue, dst, src):
+            for q in range(4):
+                queue[q].dma_start(dst[32 * q : 32 * q + 4, :].bitcast(I32), src[0, 4 * q : 4 * q + 4, :].bitcast(I32))
+
+        def deal_words(dst, src):
+            nc.vector.tensor_copy(
+                dst[:].rearrange("p (t m b) -> p t m b", t=4, b=2), src[:].rearrange("p (m t b) -> p t m b", t=4, b=2)
+            )
+
+        def deal_scales(dst, src):
+            nc.vector.tensor_copy(dst[:].rearrange("p (t m) -> p t m", t=4), src[:].rearrange("p (m t) -> p t m", t=4))
+
+        offs_t = lists.tile([P, S // 16], U16, name="offs_t")
+        n1_t = lists.tile([P, W // 16], U16, name="n1_t")
+        n2_t = lists.tile([P, W // 16], U16, name="n2_t")
+        n3_t = lists.tile([P, S // 16], U16, name="n3_t")
+        n4_t = lists.tile([P, S // 16], U16, name="n4_t")
+
+        xs = sbt([P, T], U8, "xs")
+        w1s_raw = sbt([P, S], U8, "w1s_raw")
+        w2s_raw = sbt([P, S], U8, "w2s_raw")
+        xw = sbt([P, T], I32, "xw")
+        w1w_raw = sbt([P, 2 * S], U8, "w1w_raw")
+        w2w_raw = sbt([P, 2 * S], U8, "w2w_raw")
+        gain = sbt([P, 4], F32, "gain")
+        warm_in = sbt([P, 1], F32, "warm_in")
+        warm_out = sbt([P, 1], F32, "warm_out")
+
+        nc.vector.memset(xs[:].bitcast(I32), 0)
+        nc.gpsimd.memset(w1s_raw[:].bitcast(I32), 0)
+        nc.vector.memset(warm_in[:], 0.0)
+        nc.vector.memset(w2s_raw[:].bitcast(I32), 0)
+
+        nc.sync.dma_start(offs_t[:], offs)
+        nc.scalar.dma_start(w1w_raw[:].bitcast(I32), w1_words[0].bitcast(I32))
+        nc.sync.dma_start(xw[:], x_words[0].rearrange("p n t -> p (n t)").bitcast(I32))
+        load_scale_rows([nc.scalar] * 4, xs, x_scales)
+        load_scale_rows([nc.scalar, nc.scalar, nc.gpsimd, nc.gpsimd], w1s_raw, w1_scales)
+        nc.scalar.activation(warm_out[:], warm_in[:], SIGMOID)
+        nc.sync.dma_start(n2_t[:], n2)
+        nc.sync.dma_start(n1_t[:], n1)
+        nc.sync.dma_start(gain[:], gn.rearrange("(p t) o -> p (t o)", t=4))
+        load_scale_rows([nc.sync] * 4, w2s_raw, w2_scales)
+        nc.sync.dma_start(w2w_raw[:].bitcast(I32), w2_words[0].bitcast(I32))
+        nc.sync.dma_start(n4_t[:], n4)
+        nc.sync.dma_start(n3_t[:], n3)
+
+        w1w = sbt([P, 2 * S], U8, "w1w")
+        w1s = sbt([P, S], U8, "w1s")
+        xqs = sbt([P, S], U8, "xqs")
+        deal_words(w1w, w1w_raw)
+        nc.vector.tensor_copy(xqs[:], xs[:].indirect(offs_t[:]))
+        deal_scales(w1s, w1s_raw)
+        xq = sbt([P, S], I32, "xq", tag="xs")
+        for h in range(2):
+            cols = slice(h * HALF, (h + 1) * HALF)
+            nc.vector.tensor_copy(xq[:, cols].bitcast(U32), xw[:].bitcast(U32).indirect(entries(offs_t, cols.start, cols.stop)))
+
+        def product(bank, ww, ws, t, codes, scales, cols):
+            nc.tensor.matmul_mx(
+                out=bank,
+                lhsT=ww[:, 256 * t : 256 * (t + 1)].bitcast(FP4X4),
+                lhsT_scale=ws[:, 128 * t : 128 * (t + 1)],
+                rhs=codes[:, cols].bitcast(FP8X4),
+                rhs_scale=scales[:, cols],
+                start=True,
+                stop=True,
+            )
+
+        halves = [slice(0, HALF), slice(HALF, S)]
+        whole = slice(0, S)
+        y0_ps = [ps.tile([P, HALF], F32, name=f"y0_ps{h}", tag=f"bank{h}") for h in range(2)]
+        y_ps = [None] + [ps.tile([P, S], F32, name=f"y_ps{t}", tag=f"bank{t + 1}") for t in range(1, 4)]
+        for h in range(2):
+            product(y0_ps[h][:], w1w, w1s, 0, xq, xqs, halves[h])
+        for t in range(1, 4):
+            product(y_ps[t][:], w1w, w1s, t, xq, xqs, whole)
+
+        y = [sbt([P, S], F32, f"y{t}") for t in range(4)]
+        ds = [sbt([P, S], F32, f"ds{t}") for t in range(4)]
+        pa = [sbt([P, W], F32, f"pa{t}") for t in range(4)]
+        sg = [sbt([P, W], F32, f"sg{t}") for t in range(4)]
+        z01 = sbt([P, 2, S], BF16, "z01")
+        zb = [sbt([P, HALF, 4], BF16, f"zb{h}") for h in range(2)]
+
+        def fetch_pa(t):
+            nc.vector.tensor_copy(pa[t][:], y[t][:].indirect(n1_t[:]))
+
+        def gate(t):
+            nc.scalar.activation(sg[t][:], y[t][:].indirect(n2_t[:]), SIGMOID)
+
+        def put(t):
+            nc.vector.tensor_tensor(ds[t][:].indirect(n2_t[:]), pa[t][:], sg[t][:], MULT)
+
+        def round_z(dst, t, cols):
+            nc.scalar.activation(dst, ds[t][:, cols], COPY, scale=gain[:, t : t + 1])
+
+        nc.scalar.copy(y[0][:, halves[0]], y0_ps[0][:])
+        nc.scalar.copy(ds[0][:, halves[0]], y0_ps[0][:])
+        nc.scalar.copy(y[0][:, halves[1]], y0_ps[1][:])
+        gate(0)
+        fetch_pa(0)
+        nc.vector.tensor_copy(ds[0][:, halves[1]], y[0][:, halves[1]])
+        put(0)
+        nc.scalar.copy(y[1][:], y_ps[1][:])
+        nc.scalar.copy(y[2][:], y_ps[2][:])
+        nc.sync.dma_start(ds[2][:], y[2][:])
+        gate(1)
+        nc.scalar.copy(ds[1][:], y_ps[1][:])
+        nc.scalar.copy(y[3][:], y_ps[3][:])
+        nc.sync.dma_start(ds[3][:], y[3][:])
+        fetch_pa(1)
+        fetch_pa(2)
+        put(1)
+        gate(2)
+        fetch_pa(3)
+        put(2)
+        round_z(z01[:, 0, :], 0, whole)
+        round_z(z01[:, 1, :], 1, whole)
+        gate(3)
+        put(3)
+        for h in range(2):
+            nc.scalar.copy(zb[h][:, :, 0:2], z01[:, :, halves[h]].rearrange("p t c -> p c t"))
+        for t in (2, 3):
+            for h in range(2):
+                round_z(zb[h][:, :, t], t, halves[h])
+
+        w2w = sbt([P, 2 * S], U8, "w2w", tag="pa3")
+        w2s = sbt([P, S], U8, "w2s", tag="sg3")
+        deal_words(w2w, w2w_raw)
+        deal_scales(w2s, w2s_raw)
+        zq = sbt([P, S], I32, "zq")
+        zs = sbt([P, S], U8, "zs")
+
+        def quantise_z(h):
+            nc.vector.quantize_mx(out=zq[:, halves[h]].bitcast(FP8X4), scales=zs[:, halves[h]], in_=zb[h][:].rearrange("p c t -> p (c t)"))
+
+        def fetch_y4(dst, t, h):
+            nc.vector.tensor_copy(dst, y[t][:].indirect(entries(n4_t, h * HALF, (h + 1) * HALF)))
+
+        quantise_z(0)
+        early_a = sbt([P, HALF], F32, "early_a", tag="zb0")
+        fetch_y4(early_a[:], 0, 0)
+        quantise_z(1)
+        early_b = sbt([P, 2 * HALF], F32, "early_b", tag="zb1")
+        fetch_y4(early_b[:, halves[0]], 0, 1)
+        fetch_y4(early_b[:, halves[1]], 1, 0)
+        early = {(0, 0): early_a[:], (0, 1): early_b[:, halves[0]], (1, 0): early_b[:, halves[1]]}
+
+        h0_ps = [ps.tile([P, HALF], F32, name=f"h0_ps{h}", tag=f"bank{5 + h}") for h in range(2)]
+        h_ps = [None] + [ps.tile([P, S], F32, name=f"h_ps{t}", tag=f"bank{(6 + t) % 8}") for t in range(1, 4)]
+        for h in range(2):
+            product(h0_ps[h][:], w2w, w2s, 0, zq, zs, halves[h])
+        for t in range(1, 4):
+            product(h_ps[t][:], w2w, w2s, t, zq, zs, whole)
+
+        hs = [sbt([P, S], F32, f"hs{t}") for t in range(4)]
+        for h in range(2):
+            nc.scalar.activation(hs[0][:, halves[h]], h0_ps[h][:], COPY, scale=0.75)
+        for t in range(1, 4):
+            nc.scalar.activation(hs[t][:], h_ps[t][:], COPY, scale=0.75)
+
+        out_rows = out_0.rearrange("(p t) c -> p t c", t=4)
+        out_words = out_1[0].rearrange("p n t -> p (n t)").bitcast(I32)
+        oq = sbt([P, S], I32, "oq")
+        osc = sbt([P, S], U8, "osc")
+        ob = [sbt([P, b - a, 4], BF16, f"ob{a}") for a, b in OUT_CHUNKS]
+
+        first = [sbt([P, S], F32, f"first{t}") for t in range(2)]
+        second = [sbt([P, S], F32, f"second{t}") for t in range(2)]
+        o01 = sbt([P, 2, S], F32, "o01")
+        for t in range(2):
+            for h in range(2):
+                if (t, h) in early:
+                    y_n4 = early[t, h]
+                else:
+                    y_n4 = y[t][:].indirect(entries(n4_t, h * HALF, (h + 1) * HALF))
+                nc.vector.tensor_tensor(first[t][:, halves[h]], y_n4, hs[t][:, halves[h]], MULT)
+            for h in range(2):
+                nc.vector.tensor_tensor(
+                    second[t][:, halves[h]], hs[t][:].indirect(entries(n3_t, h * HALF, (h + 1) * HALF)), y[t][:, halves[h]], MULT
+                )
+
+        def cross(i):
+            a, b = OUT_CHUNKS[i]
+            fi = sbt([P, 2, b - a], F32, f"first23_{a}")
+            se = sbt([P, 2, b - a], F32, f"second23_{a}")
+            for t in (2, 3):
+                nc.vector.tensor_tensor(fi[:, t - 2, :], y[t][:].indirect(entries(n4_t, a, b)), hs[t][:, a:b], MULT)
+                nc.vector.tensor_tensor(se[:, t - 2, :], hs[t][:].indirect(entries(n3_t, a, b)), y[t][:, a:b], MULT)
+            return fi, se
+
+        def finish(i, fi, se):
+            a, b = OUT_CHUNKS[i]
+            o23 = sbt([P, 2, b - a], F32, f"o23_{a}")
+            nc.vector.tensor_tensor(o23[:], fi[:], se[:], SUB)
+            nc.sync.dma_start(out_rows[:, 2:4, a:b], o23[:])
+            nc.scalar.copy(ob[i][:, :, 2:4], o23[:].rearrange("p t c -> p c t"))
+
+        def hand_on(i):
+            a, b = OUT_CHUNKS[i]
+            nc.vector.quantize_mx(out=oq[:, a:b].bitcast(FP8X4), scales=osc[:, a:b], in_=ob[i][:].rearrange("p c t -> p (c t)"))
+            nc.sync.dma_start(out_words[:, a:b], oq[:, a:b])
+
+        nc.vector.tensor_tensor(o01[:, 0, :], first[0][:], second[0][:], SUB)
+        nc.sync.dma_start(out_rows[:, 0, :], o01[:, 0, :])
+        c0 = cross(0)
+        nc.vector.tensor_tensor(o01[:, 1, :], first[1][:], second[1][:], SUB)
+        nc.sync.dma_start(out_rows[:, 1, :], o01[:, 1, :])
+        for i, (a, b) in enumerate(OUT_CHUNKS):
+            nc.scalar.copy(ob[i][:, :, 0:2], o01[:, :, a:b].rearrange("p t c -> p c t"))
+        c1 = cross(1)
+        finish(0, *c0)
+        c2 = cross(2)
+        finish(1, *c1)
+        hand_on(0)
+        finish(2, *c2)
+        hand_on(1)
+        hand_on(2)
+        for q in range(4):
+            queue = nc.scalar if q % 2 else nc.sync
+            queue.dma_start(out_2[0, 4 * q : 4 * q + 4, :].bitcast(I32), osc[32 * q : 32 * q + 4, :].bitcast(I32))

@@ -64,25 +64,28 @@ def tile_picked_skipcrossbfold_none_po_kernel(
         w1w_raw = sbt([P, 2 * S], U8, "w1w_raw")
         w2w_raw = sbt([P, 2 * S], U8, "w2w_raw")
         gain = sbt([P, 4], F32, "gain")
-        warm_in = sbt([P, 1], F32, "warm_in")
         warm_out = sbt([P, 1], F32, "warm_out")
 
         nc.vector.memset(xs[:].bitcast(I32), 0)
-        nc.gpsimd.memset(w1s_raw[:].bitcast(I32), 0)
-        nc.vector.memset(warm_in[:], 0.0)
+        nc.vector.memset(w1s_raw[:].bitcast(I32), 0)
         nc.vector.memset(w2s_raw[:].bitcast(I32), 0)
+        y = [sbt([P, 2 * S if t < 2 else S], F32, f"y{t}") for t in range(4)]
+        hs = [sbt([P, 2 * S if t < 2 else S], F32, f"hs{t}") for t in range(4)]
+        for t in range(2):
+            nc.vector.memset(y[t][:, S:], 0.0)
+            nc.vector.memset(hs[t][:, S:], 0.0)
 
+        nc.sync.dma_start(w1w_raw[:].bitcast(I32), w1_words[0].bitcast(I32))
         nc.sync.dma_start(offs_t[:], offs)
-        nc.scalar.dma_start(w1w_raw[:].bitcast(I32), w1_words[0].bitcast(I32))
+        load_scale_rows([nc.scalar, nc.sync, nc.scalar, nc.sync], xs, x_scales)
         nc.sync.dma_start(xw[:], x_words[0].rearrange("p n t -> p (n t)").bitcast(I32))
-        load_scale_rows([nc.scalar] * 4, xs, x_scales)
-        load_scale_rows([nc.scalar, nc.scalar, nc.gpsimd, nc.gpsimd], w1s_raw, w1_scales)
-        nc.scalar.activation(warm_out[:], warm_in[:], SIGMOID)
+        load_scale_rows([nc.scalar] * 4, w1s_raw, w1_scales)
+        nc.scalar.activation(warm_out[:], hs[1][:, S : S + 1], SIGMOID)
+        nc.sync.dma_start(w2w_raw[:].bitcast(I32), w2_words[0].bitcast(I32))
         nc.sync.dma_start(n2_t[:], n2)
         nc.sync.dma_start(n1_t[:], n1)
-        nc.sync.dma_start(gain[:], gn.rearrange("(p t) o -> p (t o)", t=4))
         load_scale_rows([nc.sync] * 4, w2s_raw, w2_scales)
-        nc.sync.dma_start(w2w_raw[:].bitcast(I32), w2_words[0].bitcast(I32))
+        nc.sync.dma_start(gain[:], gn.rearrange("(p t) o -> p (t o)", t=4))
         nc.sync.dma_start(n4_t[:], n4)
         nc.sync.dma_start(n3_t[:], n3)
 
@@ -92,18 +95,20 @@ def tile_picked_skipcrossbfold_none_po_kernel(
         deal_words(w1w, w1w_raw)
         nc.vector.tensor_copy(xqs[:], xs[:].indirect(offs_t[:]))
         deal_scales(w1s, w1s_raw)
-        xq = sbt([P, S], I32, "xq", tag="xs")
+        xq = [sbt([P, HALF], I32, "xq0", tag="xs"), sbt([P, HALF], I32, "xq1", tag="w1s_raw")]
         for h in range(2):
-            cols = slice(h * HALF, (h + 1) * HALF)
-            nc.vector.tensor_copy(xq[:, cols].bitcast(U32), xw[:].bitcast(U32).indirect(entries(offs_t, cols.start, cols.stop)))
+            nc.vector.tensor_copy(xq[h][:].bitcast(U32), xw[:].bitcast(U32).indirect(entries(offs_t, h * HALF, (h + 1) * HALF)))
 
-        def product(bank, ww, ws, t, codes, scales, cols):
+        w2w = sbt([P, 2 * S], U8, "w2w", tag="xw")
+        deal_words(w2w, w2w_raw)
+
+        def product(bank, ww, ws, t, codes, scales):
             nc.tensor.matmul_mx(
                 out=bank,
                 lhsT=ww[:, 256 * t : 256 * (t + 1)].bitcast(FP4X4),
                 lhsT_scale=ws[:, 128 * t : 128 * (t + 1)],
-                rhs=codes[:, cols].bitcast(FP8X4),
-                rhs_scale=scales[:, cols],
+                rhs=codes.bitcast(FP8X4),
+                rhs_scale=scales,
                 start=True,
                 stop=True,
             )
@@ -113,15 +118,14 @@ def tile_picked_skipcrossbfold_none_po_kernel(
         y0_ps = [ps.tile([P, HALF], F32, name=f"y0_ps{h}", tag=f"bank{h}") for h in range(2)]
         y_ps = [None] + [ps.tile([P, S], F32, name=f"y_ps{t}", tag=f"bank{t + 1}") for t in range(1, 4)]
         for h in range(2):
-            product(y0_ps[h][:], w1w, w1s, 0, xq, xqs, halves[h])
+            product(y0_ps[h][:], w1w, w1s, 0, xq[h][:], xqs[:, halves[h]])
         for t in range(1, 4):
-            product(y_ps[t][:], w1w, w1s, t, xq, xqs, whole)
+            for h in range(2):
+                product(y_ps[t][:, halves[h]], w1w, w1s, t, xq[h][:], xqs[:, halves[h]])
 
-        y = [sbt([P, S], F32, f"y{t}") for t in range(4)]
         ds = [sbt([P, S], F32, f"ds{t}") for t in range(4)]
         pa = [sbt([P, W], F32, f"pa{t}") for t in range(4)]
         sg = [sbt([P, W], F32, f"sg{t}") for t in range(4)]
-        z01 = sbt([P, 2, S], BF16, "z01")
         zb = [sbt([P, HALF, 4], BF16, f"zb{h}") for h in range(2)]
 
         def fetch_pa(t):
@@ -138,68 +142,52 @@ def tile_picked_skipcrossbfold_none_po_kernel(
 
         nc.scalar.copy(y[0][:, halves[0]], y0_ps[0][:])
         nc.scalar.copy(ds[0][:, halves[0]], y0_ps[0][:])
-        nc.scalar.copy(y[0][:, halves[1]], y0_ps[1][:])
+        nc.vector.tensor_copy(y[0][:, halves[1]], y0_ps[1][:])
         gate(0)
         fetch_pa(0)
         nc.vector.tensor_copy(ds[0][:, halves[1]], y[0][:, halves[1]])
         put(0)
-        nc.scalar.copy(y[1][:], y_ps[1][:])
-        nc.scalar.copy(y[2][:], y_ps[2][:])
-        nc.sync.dma_start(ds[2][:], y[2][:])
-        gate(1)
-        nc.scalar.copy(ds[1][:], y_ps[1][:])
-        nc.scalar.copy(y[3][:], y_ps[3][:])
-        nc.sync.dma_start(ds[3][:], y[3][:])
+        for t in range(1, 4):
+            nc.scalar.copy(y[t][:, whole], y_ps[t][:])
+            nc.sync.dma_start(ds[t][:], y[t][:, whole])
+        for t in range(1, 4):
+            gate(t)
         fetch_pa(1)
         fetch_pa(2)
         put(1)
-        gate(2)
         fetch_pa(3)
         put(2)
-        round_z(z01[:, 0, :], 0, whole)
-        round_z(z01[:, 1, :], 1, whole)
-        gate(3)
         put(3)
-        for h in range(2):
-            nc.scalar.copy(zb[h][:, :, 0:2], z01[:, :, halves[h]].rearrange("p t c -> p c t"))
-        for t in (2, 3):
+        for t in range(4):
             for h in range(2):
                 round_z(zb[h][:, :, t], t, halves[h])
 
-        w2w = sbt([P, 2 * S], U8, "w2w", tag="pa3")
         w2s = sbt([P, S], U8, "w2s", tag="sg3")
-        deal_words(w2w, w2w_raw)
         deal_scales(w2s, w2s_raw)
+        y_n4 = [sbt([P, S], F32, "y0_n4", tag="pa3")]
+        nc.vector.tensor_copy(y_n4[0][:], y[0][:].indirect(n4_t[:]))
         zq = sbt([P, S], I32, "zq")
         zs = sbt([P, S], U8, "zs")
 
         def quantise_z(h):
             nc.vector.quantize_mx(out=zq[:, halves[h]].bitcast(FP8X4), scales=zs[:, halves[h]], in_=zb[h][:].rearrange("p c t -> p (c t)"))
 
-        def fetch_y4(dst, t, h):
-            nc.vector.tensor_copy(dst, y[t][:].indirect(entries(n4_t, h * HALF, (h + 1) * HALF)))
-
         quantise_z(0)
-        early_a = sbt([P, HALF], F32, "early_a", tag="zb0")
-        fetch_y4(early_a[:], 0, 0)
         quantise_z(1)
-        early_b = sbt([P, 2 * HALF], F32, "early_b", tag="zb1")
-        fetch_y4(early_b[:, halves[0]], 0, 1)
-        fetch_y4(early_b[:, halves[1]], 1, 0)
-        early = {(0, 0): early_a[:], (0, 1): early_b[:, halves[0]], (1, 0): early_b[:, halves[1]]}
+        y_n4.append(sbt([P, S], F32, "y1_n4", tag="zb1"))
+        nc.vector.tensor_copy(y_n4[1][:], y[1][:].indirect(n4_t[:]))
 
         h0_ps = [ps.tile([P, HALF], F32, name=f"h0_ps{h}", tag=f"bank{5 + h}") for h in range(2)]
         h_ps = [None] + [ps.tile([P, S], F32, name=f"h_ps{t}", tag=f"bank{(6 + t) % 8}") for t in range(1, 4)]
         for h in range(2):
-            product(h0_ps[h][:], w2w, w2s, 0, zq, zs, halves[h])
+            product(h0_ps[h][:], w2w, w2s, 0, zq[:, halves[h]], zs[:, halves[h]])
         for t in range(1, 4):
-            product(h_ps[t][:], w2w, w2s, t, zq, zs, whole)
+            product(h_ps[t][:], w2w, w2s, t, zq[:], zs[:])
 
-        hs = [sbt([P, S], F32, f"hs{t}") for t in range(4)]
         for h in range(2):
             nc.scalar.activation(hs[0][:, halves[h]], h0_ps[h][:], COPY, scale=0.75)
         for t in range(1, 4):
-            nc.scalar.activation(hs[t][:], h_ps[t][:], COPY, scale=0.75)
+            nc.scalar.activation(hs[t][:, whole], h_ps[t][:], COPY, scale=0.75)
 
         out_rows = out_0.rearrange("(p t) c -> p t c", t=4)
         out_words = out_1[0].rearrange("p n t -> p (n t)").bitcast(I32)
@@ -207,57 +195,50 @@ def tile_picked_skipcrossbfold_none_po_kernel(
         osc = sbt([P, S], U8, "osc")
         ob = [sbt([P, b - a, 4], BF16, f"ob{a}") for a, b in OUT_CHUNKS]
 
-        first = [sbt([P, S], F32, f"first{t}") for t in range(2)]
-        second = [sbt([P, S], F32, f"second{t}") for t in range(2)]
+        first01 = sbt([P, 2, S], F32, "first01")
+        second01 = sbt([P, 2, S], F32, "second01")
         o01 = sbt([P, 2, S], F32, "o01")
-        for t in range(2):
-            for h in range(2):
-                if (t, h) in early:
-                    y_n4 = early[t, h]
-                else:
-                    y_n4 = y[t][:].indirect(entries(n4_t, h * HALF, (h + 1) * HALF))
-                nc.vector.tensor_tensor(first[t][:, halves[h]], y_n4, hs[t][:, halves[h]], MULT)
-            for h in range(2):
-                nc.vector.tensor_tensor(
-                    second[t][:, halves[h]], hs[t][:].indirect(entries(n3_t, h * HALF, (h + 1) * HALF)), y[t][:, halves[h]], MULT
-                )
+        nc.vector.tensor_tensor(second01[:, 0, :], hs[0][:].indirect(n3_t[:]), y[0][:, whole], MULT)
+        nc.vector.tensor_tensor(first01[:, 0, :], y_n4[0][:], hs[0][:, whole], MULT)
+        nc.vector.tensor_tensor(second01[:, 1, :], hs[1][:].indirect(n3_t[:]), y[1][:, whole], MULT)
+        nc.vector.tensor_tensor(first01[:, 1, :], y_n4[1][:], hs[1][:, whole], MULT)
 
-        def cross(i):
-            a, b = OUT_CHUNKS[i]
-            fi = sbt([P, 2, b - a], F32, f"first23_{a}")
-            se = sbt([P, 2, b - a], F32, f"second23_{a}")
-            for t in (2, 3):
-                nc.vector.tensor_tensor(fi[:, t - 2, :], y[t][:].indirect(entries(n4_t, a, b)), hs[t][:, a:b], MULT)
-                nc.vector.tensor_tensor(se[:, t - 2, :], hs[t][:].indirect(entries(n3_t, a, b)), y[t][:, a:b], MULT)
-            return fi, se
+        def cross(t, fi, se, a, b):
+            nc.vector.tensor_tensor(fi[:, t - 2, :], y[t][:].indirect(entries(n4_t, a, b)), hs[t][:, a:b], MULT)
+            nc.vector.tensor_tensor(se[:, t - 2, :], hs[t][:].indirect(entries(n3_t, a, b)), y[t][:, a:b], MULT)
 
-        def finish(i, fi, se):
+        def round_out(i, src, planes, a0):
             a, b = OUT_CHUNKS[i]
-            o23 = sbt([P, 2, b - a], F32, f"o23_{a}")
-            nc.vector.tensor_tensor(o23[:], fi[:], se[:], SUB)
-            nc.sync.dma_start(out_rows[:, 2:4, a:b], o23[:])
-            nc.scalar.copy(ob[i][:, :, 2:4], o23[:].rearrange("p t c -> p c t"))
+            nc.scalar.copy(
+                ob[i][:, :, planes].rearrange("p (c i) t -> p c t i", i=4),
+                src[:, :, a - a0 : b - a0].rearrange("p t (c i) -> p c t i", i=4),
+            )
 
         def hand_on(i):
             a, b = OUT_CHUNKS[i]
             nc.vector.quantize_mx(out=oq[:, a:b].bitcast(FP8X4), scales=osc[:, a:b], in_=ob[i][:].rearrange("p c t -> p (c t)"))
             nc.sync.dma_start(out_words[:, a:b], oq[:, a:b])
 
-        nc.vector.tensor_tensor(o01[:, 0, :], first[0][:], second[0][:], SUB)
-        nc.sync.dma_start(out_rows[:, 0, :], o01[:, 0, :])
-        c0 = cross(0)
-        nc.vector.tensor_tensor(o01[:, 1, :], first[1][:], second[1][:], SUB)
-        nc.sync.dma_start(out_rows[:, 1, :], o01[:, 1, :])
-        for i, (a, b) in enumerate(OUT_CHUNKS):
-            nc.scalar.copy(ob[i][:, :, 0:2], o01[:, :, a:b].rearrange("p t c -> p c t"))
-        c1 = cross(1)
-        finish(0, *c0)
-        c2 = cross(2)
-        finish(1, *c1)
-        hand_on(0)
-        finish(2, *c2)
-        hand_on(1)
-        hand_on(2)
+        cut = OUT_CHUNKS[2][0]
+        fa, sa, oa = [sbt([P, 2, cut], F32, f"{n}23a") for n in ("first", "second", "o")]
+        fb, sb_, ob_ = [sbt([P, 2, S - cut], F32, f"{n}23b") for n in ("first", "second", "o")]
+        cross(2, fa, sa, 0, cut)
+        nc.vector.tensor_tensor(o01[:], first01[:], second01[:], SUB)
+        nc.sync.dma_start(out_rows[:, 0:2, :], o01[:])
+        for i in range(3):
+            round_out(i, o01, slice(0, 2), 0)
+        cross(3, fa, sa, 0, cut)
+        cross(2, fb, sb_, cut, S)
+        nc.vector.tensor_tensor(oa[:], fa[:], sa[:], SUB)
+        nc.sync.dma_start(out_rows[:, 2:4, 0:cut], oa[:])
+        for i in range(2):
+            round_out(i, oa, slice(2, 4), 0)
+        cross(3, fb, sb_, cut, S)
+        nc.vector.tensor_tensor(ob_[:], fb[:], sb_[:], SUB)
+        nc.sync.dma_start(out_rows[:, 2:4, cut:S], ob_[:])
+        round_out(2, ob_, slice(2, 4), cut)
+        for i in range(3):
+            hand_on(i)
         for q in range(4):
             queue = nc.scalar if q % 2 else nc.sync
             queue.dma_start(out_2[0, 4 * q : 4 * q + 4, :].bitcast(I32), osc[32 * q : 32 * q + 4, :].bitcast(I32))

from contextlib import ExitStack

import concourse.mybir as mybir

F32 = mybir.dt.float32
BF16 = mybir.dt.bfloat16
I32 = mybir.dt.int32
U32 = mybir.dt.uint32
U16 = mybir.dt.uint16
U8 = mybir.dt.uint8
FP8X4 = mybir.dt.float8_e4m3fn_x4
FP4X4 = mybir.dt.float4_e2m1fn_x4
MULT = mybir.AluOpType.mult
SUB = mybir.AluOpType.subtract
COPY = mybir.ActivationFunctionType.Copy
SIGMOID = mybir.ActivationFunctionType.Sigmoid

P = 128
T = 2048
S = 512
W = 256
HALF = 256
FLOPS = 2 * 2 * 512 * 512 * 512
OUT_CHUNKS = ((0, 256), (256, 384), (384, 512))


def tile_picked_skipcrossbfold_none_po_kernel(
    tc, x_words, x_scales, w1_words, w1_scales, gn, w2_words, w2_scales, offs, n1, n2, n3, n4, out_0, out_1, out_2
):
    nc = tc.nc
    with ExitStack() as ctx:
        lists = ctx.enter_context(tc.tile_pool(name="lists", bufs=1))
        sb = ctx.enter_context(tc.tile_pool(name="sb", bufs=1))
        ps = ctx.enter_context(tc.psum_pool(name="ps", bufs=1))

        def sbt(shape, dtype, name, tag=None):
            return sb.tile(shape, dtype, name=name, tag=tag or name, align_bytes=64)

        def entries(lst, a, b):
            return lst[:, a // 16 : b // 16]

        def load_scale_rows(queue, dst, src):
            for q in range(4):
                queue[q].dma_start(dst[32 * q : 32 * q + 4, :].bitcast(I32), src[0, 4 * q : 4 * q + 4, :].bitcast(I32))

        def deal_words(dst, src):
            nc.vector.tensor_copy(
                dst[:].rearrange("p (t m b) -> p t m b", t=4, b=2), src[:].rearrange("p (m t b) -> p t m b", t=4, b=2)
            )

        def deal_scales(dst, src):
            nc.vector.tensor_copy(dst[:].rearrange("p (t m) -> p t m", t=4), src[:].rearrange("p (m t) -> p t m", t=4))

        offs_t = lists.tile([P, S // 16], U16, name="offs_t")
        n1_t = lists.tile([P, W // 16], U16, name="n1_t")
        n2_t = lists.tile([P, W // 16], U16, name="n2_t")
        n3_t = lists.tile([P, S // 16], U16, name="n3_t")
        n4_t = lists.tile([P, S // 16], U16, name="n4_t")

        xs = sbt([P, T], U8, "xs")
        w1s_raw = sbt([P, S], U8, "w1s_raw")
        w2s_raw = sbt([P, S], U8, "w2s_raw")
        xw = sbt([P, T], I32, "xw")
        w1w_raw = sbt([P, 2 * S], U8, "w1w_raw")
        w2w_raw = sbt([P, 2 * S], U8, "w2w_raw")
        gain = sbt([P, 4], F32, "gain")
        warm_out = sbt([P, 1], F32, "warm_out")

        nc.vector.memset(xs[:].bitcast(I32), 0)
        nc.vector.memset(w1s_raw[:].bitcast(I32), 0)
        nc.vector.memset(w2s_raw[:].bitcast(I32), 0)
        y = [sbt([P, 2 * S if t < 2 else S], F32, f"y{t}") for t in range(4)]
        hs = [sbt([P, 2 * S if t < 2 else S], F32, f"hs{t}") for t in range(4)]
        for t in range(2):
            nc.vector.memset(y[t][:, S:], 0.0)
            nc.vector.memset(hs[t][:, S:], 0.0)

        nc.sync.dma_start(w1w_raw[:].bitcast(I32), w1_words[0].bitcast(I32))
        nc.sync.dma_start(offs_t[:], offs)
        load_scale_rows([nc.scalar, nc.sync, nc.scalar, nc.sync], xs, x_scales)
        nc.sync.dma_start(xw[:], x_words[0].rearrange("p n t -> p (n t)").bitcast(I32))
        load_scale_rows([nc.scalar] * 4, w1s_raw, w1_scales)
        nc.scalar.activation(warm_out[:], hs[1][:, S : S + 1], SIGMOID)
        nc.sync.dma_start(w2w_raw[:].bitcast(I32), w2_words[0].bitcast(I32))
        nc.sync.dma_start(n2_t[:], n2)
        nc.sync.dma_start(n1_t[:], n1)
        load_scale_rows([nc.sync] * 4, w2s_raw, w2_scales)
        nc.sync.dma_start(gain[:], gn.rearrange("(p t) o -> p (t o)", t=4))
        nc.sync.dma_start(n4_t[:], n4)
        nc.sync.dma_start(n3_t[:], n3)

        w1w = sbt([P, 2 * S], U8, "w1w")
        w1s = sbt([P, S], U8, "w1s")
        xqs = sbt([P, S], U8, "xqs")
        deal_words(w1w, w1w_raw)
        nc.vector.tensor_copy(xqs[:], xs[:].indirect(offs_t[:]))
        deal_scales(w1s, w1s_raw)
        xq = [sbt([P, HALF], I32, "xq0", tag="xs"), sbt([P, HALF], I32, "xq1", tag="w1s_raw")]
        for h in range(2):
            nc.vector.tensor_copy(xq[h][:].bitcast(U32), xw[:].bitcast(U32).indirect(entries(offs_t, h * HALF, (h + 1) * HALF)))

        w2w = sbt([P, 2 * S], U8, "w2w", tag="xw")
        deal_words(w2w, w2w_raw)

        def product(bank, ww, ws, t, codes, scales):
            nc.tensor.matmul_mx(
                out=bank,
                lhsT=ww[:, 256 * t : 256 * (t + 1)].bitcast(FP4X4),
                lhsT_scale=ws[:, 128 * t : 128 * (t + 1)],
                rhs=codes.bitcast(FP8X4),
                rhs_scale=scales,
                start=True,
                stop=True,
            )

        halves = [slice(0, HALF), slice(HALF, S)]
        whole = slice(0, S)
        y0_ps = [ps.tile([P, HALF], F32, name=f"y0_ps{h}", tag=f"bank{h}") for h in range(2)]
        y_ps = [None] + [ps.tile([P, S], F32, name=f"y_ps{t}", tag=f"bank{t + 1}") for t in range(1, 4)]
        for h in range(2):
            product(y0_ps[h][:], w1w, w1s, 0, xq[h][:], xqs[:, halves[h]])
        for t in range(1, 4):
            for h in range(2):
                product(y_ps[t][:, halves[h]], w1w, w1s, t, xq[h][:], xqs[:, halves[h]])

        ds = [sbt([P, S], F32, f"ds{t}") for t in range(4)]
        pa = [sbt([P, W], F32, f"pa{t}") for t in range(4)]
        sg = [sbt([P, W], F32, f"sg{t}") for t in range(4)]
        zb = [sbt([P, HALF, 4], BF16, f"zb{h}") for h in range(2)]

        def fetch_pa(t):
            nc.vector.tensor_copy(pa[t][:], y[t][:].indirect(n1_t[:]))

        def gate(t):
            nc.scalar.activation(sg[t][:], y[t][:].indirect(n2_t[:]), SIGMOID)

        def put(t):
            nc.vector.tensor_tensor(ds[t][:].indirect(n2_t[:]), pa[t][:], sg[t][:], MULT)

        def round_z(dst, t, cols):
            nc.scalar.activation(dst, ds[t][:, cols], COPY, scale=gain[:, t : t + 1])

        nc.scalar.copy(y[0][:, halves[0]], y0_ps[0][:])
        nc.scalar.copy(ds[0][:, halves[0]], y0_ps[0][:])
        nc.vector.tensor_copy(y[0][:, halves[1]], y0_ps[1][:])
        gate(0)
        fetch_pa(0)
        nc.vector.tensor_copy(ds[0][:, halves[1]], y[0][:, halves[1]])
        put(0)
        for t in range(1, 4):
            nc.scalar.copy(y[t][:, whole], y_ps[t][:])
            nc.sync.dma_start(ds[t][:], y[t][:, whole])
        for t in range(1, 4):
            gate(t)
        fetch_pa(1)
        fetch_pa(2)
        put(1)
        fetch_pa(3)
        put(2)
        put(3)
        for t in range(4):
            for h in range(2):
                round_z(zb[h][:, :, t], t, halves[h])

        w2s = sbt([P, S], U8, "w2s", tag="sg3")
        deal_scales(w2s, w2s_raw)
        y_n4 = [sbt([P, S], F32, "y0_n4", tag="pa3")]
        nc.vector.tensor_copy(y_n4[0][:], y[0][:].indirect(n4_t[:]))
        zq = sbt([P, S], I32, "zq")
        zs = sbt([P, S], U8, "zs")

        def quantise_z(h):
            nc.vector.quantize_mx(out=zq[:, halves[h]].bitcast(FP8X4), scales=zs[:, halves[h]], in_=zb[h][:].rearrange("p c t -> p (c t)"))

        quantise_z(0)
        quantise_z(1)
        y_n4.append(sbt([P, S], F32, "y1_n4", tag="zb1"))
        nc.vector.tensor_copy(y_n4[1][:], y[1][:].indirect(n4_t[:]))

        h0_ps = [ps.tile([P, HALF], F32, name=f"h0_ps{h}", tag=f"bank{5 + h}") for h in range(2)]
        h_ps = [None] + [ps.tile([P, S], F32, name=f"h_ps{t}", tag=f"bank{(6 + t) % 8}") for t in range(1, 4)]
        for h in range(2):
            product(h0_ps[h][:], w2w, w2s, 0, zq[:, halves[h]], zs[:, halves[h]])
        for t in range(1, 4):
            product(h_ps[t][:], w2w, w2s, t, zq[:], zs[:])

        for h in range(2):
            nc.scalar.activation(hs[0][:, halves[h]], h0_ps[h][:], COPY, scale=0.75)
        for t in range(1, 4):
            nc.scalar.activation(hs[t][:, whole], h_ps[t][:], COPY, scale=0.75)

        out_rows = out_0.rearrange("(p t) c -> p t c", t=4)
        out_words = out_1[0].rearrange("p n t -> p (n t)").bitcast(I32)
        oq = sbt([P, S], I32, "oq")
        osc = sbt([P, S], U8, "osc")
        ob = [sbt([P, b - a, 4], BF16, f"ob{a}") for a, b in OUT_CHUNKS]

        first01 = sbt([P, 2, S], F32, "first01")
        second01 = sbt([P, 2, S], F32, "second01")
        o01 = sbt([P, 2, S], F32, "o01")
        nc.vector.tensor_tensor(second01[:, 0, :], hs[0][:].indirect(n3_t[:]), y[0][:, whole], MULT)
        nc.vector.tensor_tensor(first01[:, 0, :], y_n4[0][:], hs[0][:, whole], MULT)
        nc.vector.tensor_tensor(second01[:, 1, :], hs[1][:].indirect(n3_t[:]), y[1][:, whole], MULT)
        nc.vector.tensor_tensor(first01[:, 1, :], y_n4[1][:], hs[1][:, whole], MULT)

        def cross(t, fi, se, a, b):
            nc.vector.tensor_tensor(fi[:, t - 2, :], y[t][:].indirect(entries(n4_t, a, b)), hs[t][:, a:b], MULT)
            nc.vector.tensor_tensor(se[:, t - 2, :], hs[t][:].indirect(entries(n3_t, a, b)), y[t][:, a:b], MULT)

        def round_out(i, src, planes, a0):
            a, b = OUT_CHUNKS[i]
            nc.scalar.copy(
                ob[i][:, :, planes].rearrange("p (c i) t -> p c t i", i=4),
                src[:, :, a - a0 : b - a0].rearrange("p t (c i) -> p c t i", i=4),
            )

        def hand_on(i):
            a, b = OUT_CHUNKS[i]
            nc.vector.quantize_mx(out=oq[:, a:b].bitcast(FP8X4), scales=osc[:, a:b], in_=ob[i][:].rearrange("p c t -> p (c t)"))
            nc.sync.dma_start(out_words[:, a:b], oq[:, a:b])

        cut = OUT_CHUNKS[2][0]
        fa, sa, oa = [sbt([P, 2, cut], F32, f"{n}23a") for n in ("first", "second", "o")]
        fb, sb_, ob_ = [sbt([P, 2, S - cut], F32, f"{n}23b") for n in ("first", "second", "o")]
        cross(2, fa, sa, 0, cut)
        nc.vector.tensor_tensor(o01[:], first01[:], second01[:], SUB)
        nc.sync.dma_start(out_rows[:, 0:2, :], o01[:])
        for i in range(3):
            round_out(i, o01, slice(0, 2), 0)
        cross(3, fa, sa, 0, cut)
        cross(2, fb, sb_, cut, S)
        nc.vector.tensor_tensor(oa[:], fa[:], sa[:], SUB)
        nc.sync.dma_start(out_rows[:, 2:4, 0:cut], oa[:])
        for i in range(2):
            round_out(i, oa, slice(2, 4), 0)
        cross(3, fb, sb_, cut, S)
        nc.vector.tensor_tensor(ob_[:], fb[:], sb_[:], SUB)
        nc.sync.dma_start(out_rows[:, 2:4, cut:S], ob_[:])
        round_out(2, ob_, slice(2, 4), cut)
        for i in range(3):
            hand_on(i)
        for q in range(4):
            queue = nc.scalar if q % 2 else nc.sync
            queue.dma_start(out_2[0, 4 * q : 4 * q + 4, :].bitcast(I32), osc[32 * q : 32 * q + 4, :].bitcast(I32))
